import numpy as np
import ml_dtypes


def mxq(x, axis, fmt="e4m3"):
    dtype, down = {"e4m3": (ml_dtypes.float8_e4m3fn, 7), "e5m2": (ml_dtypes.float8_e5m2, 14)}[fmt]
    v = np.moveaxis(np.asarray(x, np.float32).astype(ml_dtypes.bfloat16).astype(np.float64), axis, -1)
    blocks = v.reshape(v.shape[:-1] + (-1, 32))
    amax = np.abs(blocks).max(-1, keepdims=True)
    byte = np.maximum(np.where(amax > 0, np.frexp(amax)[1] - 1 + 127, 0) - down, 1)
    scale = np.exp2(byte - 127.0)
    codes = (blocks / scale).astype(np.float32).astype(dtype).astype(np.float64)
    return np.moveaxis((codes * scale).reshape(v.shape), -1, axis)


WIDE = False


def mx_kscale(k):
    if not WIDE:
        return np.ones(k)
    levels = np.array([10, -10, 5, -5, 0])
    if k % 512:
        return np.exp2(np.random.permutation(np.resize(levels, k // 32))).repeat(32)
    a = np.empty((k // 512, 16))
    for p in range(k // 512):
        a[p, :8] = np.random.permutation(np.resize(levels, 8))
        for g in range(8):
            far = levels[np.abs(levels - a[p, g]) >= 10]
            a[p, g + 8] = far[np.random.randint(len(far))]
    return np.exp2(a.ravel()).repeat(32)


def f64(x):
    return np.asarray(x).astype(np.float64)


def striped(idx):
    return np.tile(idx.reshape(-1, 16).T, (8, 1)).astype(np.uint16)


def unstriped(offs):
    return offs[:16].T.reshape(-1).astype(np.int64)


def pack_weight(w):
    k, n = w.shape
    w = f64(np.asarray(w, np.float32).astype(ml_dtypes.bfloat16)).reshape(k // 32, 32, n)
    amax = np.abs(w).max(1)
    byte = np.clip(np.where(amax > 0, np.frexp(amax)[1] - 1 + 127 - 7, 1), 1, 254)
    scaled = (w * np.exp2(127.0 - byte)[:, None, :]).reshape(k, n).astype(np.float32)
    words = np.ascontiguousarray(scaled.reshape(k // 512, 128, 4, n).transpose(0, 1, 3, 2)).astype(ml_dtypes.float8_e4m3fn).view(np.uint8)
    return words, np.ascontiguousarray(byte.astype(np.uint8).reshape(k // 512, 16, n))


def unpack_weight(words, scales):
    g, p, n, _ = words.shape
    vals = np.ascontiguousarray(words).view(ml_dtypes.float8_e4m3fn).astype(np.float64) * np.repeat(np.exp2(scales.astype(np.float64) - 127.0), 8, axis=1)[..., None]
    return vals.transpose(0, 1, 3, 2).reshape(g * 512, n)


K, T, S, N, H = 1024, 1024, 512, 128, 512


def setup_inputs():
    n = np.random.standard_normal
    s = mx_kscale(K)[:, None]
    u = mx_kscale(H)
    packed_xT = pack_weight(n((K, T)) * s)
    return {
        "x_words": packed_xT[0],
        "x_scales": packed_xT[1],
        "w1": (n((K, H)) / np.sqrt(K) / s).astype(np.float32),
        "w2": (n((K, H)) / np.sqrt(K) / s).astype(np.float32),
        "unit": (np.random.uniform(0.6, 1.4, (H, 1)) * u[:, None]).astype(np.float32),
        "w3": (n((H, N)) / np.sqrt(H) / u[:, None]).astype(np.float32),
        "offs": striped(np.random.permutation(T)[:S]),
        "u1": striped(np.random.permutation(S)),
        "u2": striped(np.random.permutation(S)),
    }


def reference(x_words, x_scales, w1, w2, unit, w3, offs, u1, u2):
    xq = unpack_weight(x_words, x_scales)[:, unstriped(offs)]
    y = mxq(f64(w1), 0, "e4m3").T @ xq
    d0 = np.log(np.exp(y) + 1.0)
    da = d0[:, unstriped(u1)]
    yw = mxq(f64(w2), 0, "e4m3").T @ xq
    wgt = np.log(np.exp(yw) + 1.0)
    d1 = np.minimum(d0, da + 0.4 * wgt)
    db = d1[:, unstriped(u2)]
    cu = wgt[:, unstriped(u1)]
    d2 = np.minimum(d1, db + 0.4 * cu)
    impr = d0 - d2
    hid = f64(unit) * (d2 - (0.5 * impr))
    return mxq(f64(w3), 0, "e4m3").T @ mxq(hid, 0, "e4m3")

@@ -1,0 +1,232 @@
+from contextlib import ExitStack
+
+import concourse.mybir as mybir
+
+K, T, S, N, H = 1024, 1024, 512, 128, 512
+FLOPS = 2 * (2 * K * H * S + H * N * S)
+
+F32 = mybir.dt.float32
+BF16 = mybir.dt.bfloat16
+I32 = mybir.dt.int32
+U32 = mybir.dt.uint32
+U16 = mybir.dt.uint16
+U8 = mybir.dt.uint8
+FP8X4 = mybir.dt.float8_e4m3fn_x4
+ALU = mybir.AluOpType
+ACT = mybir.ActivationFunctionType
+
+P = 128
+PACK = 4
+K_PASS = P * PACK
+PASSES = K // K_PASS
+LIST = 16
+HALF = S // 2
+SPLIT = 64
+LN_FLOOR = 2.0**-62
+TAIL = ((0, 256), (256, 384), (384, 512))
+
+
+def tile_picked_ybellmf_dist_p_kernel(
+    tc, x_words, x_scales, w1, w2, unit, w3, offs, u1, u2, out
+):
+    nc = tc.nc
+    with ExitStack() as ctx:
+        keep = ctx.enter_context(tc.tile_pool(name="keep", bufs=1))
+        psum = ctx.enter_context(tc.psum_pool(name="psum", bufs=1))
+
+        def load_list(name, src):
+            tile = keep.tile([P, S // LIST], U16, name=name)
+            nc.sync.dma_start(tile[:], src)
+            return tile
+
+        def load_words(g):
+            tile = keep.tile([P, T], I32, name=f"x_all{g}")
+            nc.sync.dma_start(tile[:], x_words[g].rearrange("p n r -> p (n r)").bitcast(I32))
+            return tile
+
+        def load_weight(name, w, g, c0, c1):
+            tile = keep.tile([P, PACK, c1 - c0], F32, name=name)
+            rows = w[g * K_PASS : (g + 1) * K_PASS, c0:c1]
+            nc.sync.dma_start(tile[:], rows.rearrange("(p j) c -> p j c", j=PACK))
+            return tile
+
+        xs_all = keep.tile([P, T], U8, name="xs_all")
+        xs_rows = keep.tile([P, T // 4], I32, name="xs_rows")
+        nc.vector.memset(xs_all[:].bitcast(I32), 0)
+        unit_sb = keep.tile([P, PACK], F32, name="unit_sb")
+
+        w1_0a = load_weight("w1_0a", w1, 0, 0, H // 2)
+        for q in range(4):
+            rows = slice(32 * q, 32 * q + 4 * PASSES)
+            nc.sync.dma_start(xs_rows[rows, :], x_scales[:, 4 * q : 4 * q + 4, :].bitcast(I32))
+            nc.vector.tensor_copy(xs_all[rows, :].bitcast(I32), xs_rows[rows, :])
+        offs_sb = load_list("offs_sb", offs)
+        w1_0b = load_weight("w1_0b", w1, 0, H // 2, H)
+        x_all0 = load_words(0)
+        x_all1 = load_words(1)
+        w1_1a = load_weight("w1_1a", w1, 1, 0, H // 2)
+        w1_1b = load_weight("w1_1b", w1, 1, H // 2, H)
+        w3_raw = load_weight("w3_raw", w3, 0, 0, N)
+        w2_0a = load_weight("w2_0a", w2, 0, 0, H // 2)
+        w2_0b = load_weight("w2_0b", w2, 0, H // 2, H)
+        w2_1 = load_weight("w2_1", w2, 1, 0, H)
+        nc.sync.dma_start(unit_sb[:], unit.rearrange("(p t) o -> p (t o)", t=PACK))
+        u1_sb = load_list("u1_sb", u1)
+        u2_sb = load_list("u2_sb", u2)
+
+        def deal(copy, grouped, raw, c0):
+            m0, m1 = c0 // PACK, (c0 + raw.shape[2]) // PACK
+            copy(
+                grouped[:, :, m0:m1, :].rearrange("p t m j -> p m j t"),
+                raw.rearrange("p j (m t) -> p m j t", t=PACK),
+            )
+
+        def grouped_tile(name):
+            return keep.tile([P, PACK, P, PACK], BF16, name=name, align_bytes=64)
+
+        def quantize(name, src):
+            width = src.shape[1] // PACK
+            codes = keep.tile([P, width], U32, name=name + "_codes", align_bytes=64)
+            scales = keep.tile([P, width], U8, name=name + "_scales", align_bytes=64)
+            nc.vector.quantize_mx(out=codes[:].bitcast(FP8X4), scales=scales[:], in_=src)
+            return codes, scales
+
+        x_codes = []
+        x_sc = keep.tile([P, S], U8, name="x_sc", align_bytes=64)
+
+        def gather_words(g, x_all):
+            tile = keep.tile([P, S], U32, name=f"x_codes{g}", align_bytes=64)
+            nc.vector.tensor_copy(tile[:], x_all[:].bitcast(U32).indirect(offs_sb[:]))
+            x_codes.append(tile)
+
+        def product(bank, codes, scales, g):
+            nc.tensor.matmul_mx(
+                out=bank[:],
+                lhsT=codes.bitcast(FP8X4),
+                lhsT_scale=scales,
+                rhs=x_codes[g][:].bitcast(FP8X4),
+                rhs_scale=x_sc[4 * g : P, :],
+                start=(g == 0),
+                stop=(g == PASSES - 1),
+            )
+
+        def first_pass(name, grouped, banks):
+            codes, scales = quantize(name, grouped[:].rearrange("p t m j -> p (t m j)"))
+            for t in range(PACK):
+                product(banks[t], codes[:, t * P : (t + 1) * P], scales[:, t * P : (t + 1) * P], 0)
+
+        def second_pass(name, grouped, banks):
+            for t in range(PACK):
+                codes, scales = quantize(f"{name}_{t}", grouped[:, t].rearrange("p m j -> p (m j)"))
+                product(banks[t], codes[:], scales[:], 1)
+
+        def log_sigmoid(name, banks):
+            sig = keep.tile([P, PACK, S], F32, name=name + "_sig")
+            log = keep.tile([P, PACK, S], F32, name=name + "_log")
+            for t in range(PACK):
+                nc.scalar.activation(sig[:, t, :], banks[t][:], ACT.Sigmoid, scale=-1.0)
+            for t in range(PACK):
+                nc.scalar.activation(log[:, t, :], sig[:, t, :], ACT.Ln, bias=LN_FLOOR)
+            return log
+
+        def softplus(dst, log, bank):
+            nc.vector.scalar_tensor_tensor(dst, log, -1.0, bank[:], ALU.mult, ALU.max)
+
+        def entries(lst, j0, j1):
+            return lst[:, j0 // LIST : j1 // LIST]
+
+        y = [psum.tile([P, S], F32, name=f"y{t}", tag=f"bank{t}") for t in range(PACK)]
+        yw = [psum.tile([P, S], F32, name=f"yw{t}", tag=f"bank{PACK + t}") for t in range(PACK)]
+        nc.vector.tensor_copy(x_sc[:], xs_all[:].indirect(offs_sb[:]))
+        g10 = grouped_tile("g10")
+        deal(nc.scalar.copy, g10, w1_0a[:], 0)
+        deal(nc.scalar.copy, g10, w1_0b[:, :, :SPLIT], H // 2)
+        deal(nc.vector.tensor_copy, g10, w1_0b[:, :, SPLIT:], H // 2 + SPLIT)
+        gather_words(0, x_all0)
+        first_pass("q10", g10, y)
+        gather_words(1, x_all1)
+        g11 = grouped_tile("g11")
+        deal(nc.scalar.copy, g11, w1_1a[:], 0)
+        deal(nc.scalar.copy, g11, w1_1b[:, :, :SPLIT], H // 2)
+        deal(nc.vector.tensor_copy, g11, w1_1b[:, :, SPLIT:], H // 2 + SPLIT)
+        second_pass("q11", g11, y)
+        log_y = log_sigmoid("y", y)
+
+        g3 = keep.tile([P, N, PACK], BF16, name="g3", align_bytes=64)
+        nc.vector.tensor_copy(
+            g3[:].rearrange("p (c i) j -> p c j i", i=4),
+            w3_raw[:].rearrange("p j (c i) -> p c j i", i=4),
+        )
+        w3_codes, w3_scales = quantize("q3", g3[:].rearrange("p n j -> p (n j)"))
+        unit15 = keep.tile([P, PACK], F32, name="unit15")
+        nc.vector.tensor_scalar(unit15[:], unit_sb[:], 1.5, None, ALU.mult)
+
+        g20 = grouped_tile("g20")
+        deal(nc.vector.tensor_copy, g20, w2_0a[:], 0)
+        deal(nc.vector.tensor_copy, g20, w2_0b[:], H // 2)
+        first_pass("q20", g20, yw)
+        g21 = grouped_tile("g21")
+        deal(nc.vector.tensor_copy, g21, w2_1[:], 0)
+        second_pass("q21", g21, yw)
+
+        d0 = [keep.tile([P, S], F32, name=f"d0_{t}") for t in range(PACK)]
+        da = keep.tile([P, PACK, S], F32, name="da")
+        d0u = keep.tile([P, PACK, S], F32, name="d0u")
+        for t in range(PACK):
+            softplus(d0[t][:], log_y[:, t, :], y[t])
+        for t in range(PACK):
+            for j0 in (0, HALF):
+                nc.vector.tensor_copy(da[:, t, j0 : j0 + HALF], d0[t][:].indirect(entries(u1_sb, j0, j0 + HALF)))
+        for t in range(PACK):
+            nc.vector.tensor_scalar(d0u[:, t, :], d0[t][:], unit_sb[:, t : t + 1], 0.5, ALU.mult, ALU.mult)
+
+        log_w = log_sigmoid("yw", yw)
+        wgt = [keep.tile([P, S], F32, name=f"wgt_{t}") for t in range(PACK)]
+        via1 = keep.tile([P, PACK, S], F32, name="via1")
+        d1 = keep.tile([P, PACK, S], F32, name="d1")
+        for pair in ((0, 1), (2, 3)):
+            for t in pair:
+                softplus(wgt[t][:], log_w[:, t, :], yw[t])
+            for t in pair:
+                nc.vector.scalar_tensor_tensor(via1[:, t, :], wgt[t][:], 0.4, da[:, t, :], ALU.mult, ALU.add)
+            for t in pair:
+                nc.vector.tensor_tensor(d1[:, t, :], via1[:, t, :], d0[t][:], ALU.min)
+
+        for n, (j0, j1) in enumerate(TAIL):
+            width = j1 - j0
+            cu4 = keep.tile([P, PACK, width], F32, name=f"cu4_{n}")
+            db = keep.tile([P, PACK, width], F32, name=f"db{n}")
+            via2 = keep.tile([P, PACK, width], F32, name=f"via2_{n}")
+            d2 = keep.tile([P, PACK, width], F32, name=f"d2_{n}")
+            hid = keep.tile([P, PACK, width], BF16, name=f"hid{n}")
+            hid_g = keep.tile([P, width, PACK], BF16, name=f"hid_g{n}", align_bytes=64)
+            res = keep.tile([P, width], F32, name=f"res{n}")
+            for t in range(PACK):
+                nc.scalar.activation(cu4[:, t, :], wgt[t][:].indirect(entries(u1_sb, j0, j1)), ACT.Copy, scale=0.4)
+            for t in range(PACK):
+                nc.scalar.activation(db[:, t, :], d1[:, t, :].indirect(entries(u2_sb, j0, j1)), ACT.Copy)
+            for a in (0, 2):
+                nc.vector.tensor_tensor(via2[:, a : a + 2], db[:, a : a + 2], cu4[:, a : a + 2], ALU.add)
+            for a in (0, 2):
+                nc.vector.tensor_tensor(d2[:, a : a + 2], via2[:, a : a + 2], d1[:, a : a + 2, j0:j1], ALU.min)
+            for t in range(PACK):
+                nc.vector.scalar_tensor_tensor(
+                    hid[:, t, :], d2[:, t, :], unit15[:, t : t + 1], d0u[:, t, j0:j1], ALU.mult, ALU.subtract
+                )
+            nc.scalar.copy(
+                hid_g[:].rearrange("p (c i) t -> p c t i", i=4),
+                hid[:].rearrange("p t (c i) -> p c t i", i=4),
+            )
+            h_codes, h_scales = quantize(f"qh{n}", hid_g[:].rearrange("p c t -> p (c t)"))
+            acc = psum.tile([P, width], F32, name=f"acc{n}", tag=f"bank{n}")
+            nc.tensor.matmul_mx(
+                out=acc[:],
+                lhsT=w3_codes[:].bitcast(FP8X4),
+                lhsT_scale=w3_scales[:],
+                rhs=h_codes[:].bitcast(FP8X4),
+                rhs_scale=h_scales[:],
+                start=True,
+                stop=True,
+            )
+            nc.scalar.copy(res[:], acc[:])
+            nc.sync.dma_start(out[:, j0:j1], res[:])

@@ -21,7 +21,7 @@ K_PASS = P * PACK
 PASSES = K // K_PASS
 LIST = 16
 HALF = S // 2
-SPLIT = 64
+SPLIT = 96
 LN_FLOOR = 2.0**-62
 TAIL = ((0, 256), (256, 384), (384, 512))
 
@@ -44,8 +44,8 @@ def tile_picked_ybellmf_dist_p_kernel(
             nc.sync.dma_start(tile[:], x_words[g].rearrange("p n r -> p (n r)").bitcast(I32))
             return tile
 
-        def load_weight(name, w, g, c0, c1):
-            tile = keep.tile([P, PACK, c1 - c0], F32, name=name)
+        def load_weight(name, w, g, c0, c1, tag=None):
+            tile = keep.tile([P, PACK, c1 - c0], F32, name=name, tag=tag or name)
             rows = w[g * K_PASS : (g + 1) * K_PASS, c0:c1]
             nc.sync.dma_start(tile[:], rows.rearrange("(p j) c -> p j c", j=PACK))
             return tile
@@ -55,21 +55,21 @@ def tile_picked_ybellmf_dist_p_kernel(
         nc.vector.memset(xs_all[:].bitcast(I32), 0)
         unit_sb = keep.tile([P, PACK], F32, name="unit_sb")
 
-        w1_0a = load_weight("w1_0a", w1, 0, 0, H // 2)
         for q in range(4):
             rows = slice(32 * q, 32 * q + 4 * PASSES)
             nc.sync.dma_start(xs_rows[rows, :], x_scales[:, 4 * q : 4 * q + 4, :].bitcast(I32))
             nc.vector.tensor_copy(xs_all[rows, :].bitcast(I32), xs_rows[rows, :])
         offs_sb = load_list("offs_sb", offs)
-        w1_0b = load_weight("w1_0b", w1, 0, H // 2, H)
+        w1_0a = load_weight("w1_0a", w1, 0, 0, H // 2)
         x_all0 = load_words(0)
+        w1_0b = load_weight("w1_0b", w1, 0, H // 2, H)
         x_all1 = load_words(1)
         w1_1a = load_weight("w1_1a", w1, 1, 0, H // 2)
         w1_1b = load_weight("w1_1b", w1, 1, H // 2, H)
-        w3_raw = load_weight("w3_raw", w3, 0, 0, N)
         w2_0a = load_weight("w2_0a", w2, 0, 0, H // 2)
         w2_0b = load_weight("w2_0b", w2, 0, H // 2, H)
-        w2_1 = load_weight("w2_1", w2, 1, 0, H)
+        w2_1a = load_weight("w2_1a", w2, 1, 0, H // 2)
+        w2_1b = load_weight("w2_1b", w2, 1, H // 2, H)
         nc.sync.dma_start(unit_sb[:], unit.rearrange("(p t) o -> p (t o)", t=PACK))
         u1_sb = load_list("u1_sb", u1)
         u2_sb = load_list("u2_sb", u2)
@@ -140,34 +140,32 @@ def tile_picked_ybellmf_dist_p_kernel(
         nc.vector.tensor_copy(x_sc[:], xs_all[:].indirect(offs_sb[:]))
         g10 = grouped_tile("g10")
         deal(nc.scalar.copy, g10, w1_0a[:], 0)
+        gather_words(0, x_all0)
         deal(nc.scalar.copy, g10, w1_0b[:, :, :SPLIT], H // 2)
         deal(nc.vector.tensor_copy, g10, w1_0b[:, :, SPLIT:], H // 2 + SPLIT)
-        gather_words(0, x_all0)
         first_pass("q10", g10, y)
         gather_words(1, x_all1)
         g11 = grouped_tile("g11")
-        deal(nc.scalar.copy, g11, w1_1a[:], 0)
-        deal(nc.scalar.copy, g11, w1_1b[:, :, :SPLIT], H // 2)
-        deal(nc.vector.tensor_copy, g11, w1_1b[:, :, SPLIT:], H // 2 + SPLIT)
+        deal(nc.scalar.copy, g11, w1_1a[:, :, :SPLIT], 0)
+        deal(nc.vector.tensor_copy, g11, w1_1a[:, :, SPLIT:], SPLIT)
+        deal(nc.vector.tensor_copy, g11, w1_1b[:], H // 2)
         second_pass("q11", g11, y)
         log_y = log_sigmoid("y", y)
-
-        g3 = keep.tile([P, N, PACK], BF16, name="g3", align_bytes=64)
-        nc.vector.tensor_copy(
-            g3[:].rearrange("p (c i) j -> p c j i", i=4),
-            w3_raw[:].rearrange("p j (c i) -> p c j i", i=4),
-        )
-        w3_codes, w3_scales = quantize("q3", g3[:].rearrange("p n j -> p (n j)"))
-        unit15 = keep.tile([P, PACK], F32, name="unit15")
-        nc.vector.tensor_scalar(unit15[:], unit_sb[:], 1.5, None, ALU.mult)
 
         g20 = grouped_tile("g20")
         deal(nc.vector.tensor_copy, g20, w2_0a[:], 0)
         deal(nc.vector.tensor_copy, g20, w2_0b[:], H // 2)
         first_pass("q20", g20, yw)
         g21 = grouped_tile("g21")
-        deal(nc.vector.tensor_copy, g21, w2_1[:], 0)
+        deal(nc.vector.tensor_copy, g21, w2_1a[:], 0)
+        deal(nc.vector.tensor_copy, g21, w2_1b[:], H // 2)
         second_pass("q21", g21, yw)
+        w3_raw = load_weight("w3_raw", w3, 0, 0, N, tag="w2_1b")
+
+        unit15 = keep.tile([P, PACK], F32, name="unit15")
+        nc.vector.tensor_scalar(unit15[:], unit_sb[:], 1.5, None, ALU.mult)
+        unit05 = keep.tile([P, PACK], F32, name="unit05")
+        nc.vector.tensor_scalar(unit05[:], unit_sb[:], 0.5, None, ALU.mult)
 
         d0 = [keep.tile([P, S], F32, name=f"d0_{t}") for t in range(PACK)]
         da = keep.tile([P, PACK, S], F32, name="da")
@@ -178,13 +176,19 @@ def tile_picked_ybellmf_dist_p_kernel(
             for j0 in (0, HALF):
                 nc.vector.tensor_copy(da[:, t, j0 : j0 + HALF], d0[t][:].indirect(entries(u1_sb, j0, j0 + HALF)))
         for t in range(PACK):
-            nc.vector.tensor_scalar(d0u[:, t, :], d0[t][:], unit_sb[:, t : t + 1], 0.5, ALU.mult, ALU.mult)
+            nc.gpsimd.tensor_scalar(d0u[:, t, :], d0[t][:], unit05[:, t : t + 1], 0.0, ALU.mult, ALU.add)
 
         log_w = log_sigmoid("yw", yw)
         wgt = [keep.tile([P, S], F32, name=f"wgt_{t}") for t in range(PACK)]
         via1 = keep.tile([P, PACK, S], F32, name="via1")
         d1 = keep.tile([P, PACK, S], F32, name="d1")
-        for pair in ((0, 1), (2, 3)):
+        cu4 = keep.tile([P, PACK, S], F32, name="cu4")
+        db = keep.tile([P, PACK, S], F32, name="db")
+        via2 = keep.tile([P, PACK, S], F32, name="via2")
+        d2 = keep.tile([P, PACK, S], F32, name="d2")
+        hid = keep.tile([P, PACK, S], BF16, name="hid")
+
+        def first_round(pair):
             for t in pair:
                 softplus(wgt[t][:], log_w[:, t, :], yw[t])
             for t in pair:
@@ -192,30 +196,48 @@ def tile_picked_ybellmf_dist_p_kernel(
             for t in pair:
                 nc.vector.tensor_tensor(d1[:, t, :], via1[:, t, :], d0[t][:], ALU.min)
 
+        def fetch(pair, j0, j1):
+            for t in pair:
+                nc.scalar.activation(cu4[:, t, j0:j1], wgt[t][:].indirect(entries(u1_sb, j0, j1)), ACT.Copy, scale=0.4)
+            for t in pair:
+                nc.scalar.activation(db[:, t, j0:j1], d1[:, t, :].indirect(entries(u2_sb, j0, j1)), ACT.Copy)
+
+        def second_round(pair, j0, j1):
+            for t in pair:
+                nc.vector.tensor_tensor(via2[:, t, j0:j1], db[:, t, j0:j1], cu4[:, t, j0:j1], ALU.add)
+            for t in pair:
+                nc.vector.tensor_tensor(d2[:, t, j0:j1], via2[:, t, j0:j1], d1[:, t, j0:j1], ALU.min)
+            for t in pair:
+                nc.vector.scalar_tensor_tensor(
+                    hid[:, t, j0:j1], d2[:, t, j0:j1], unit15[:, t : t + 1], d0u[:, t, j0:j1], ALU.mult, ALU.subtract
+                )
+
+        g3 = keep.tile([P, N, PACK], BF16, name="g3", align_bytes=64)
+        nc.gpsimd.tensor_scalar(
+            g3[:].rearrange("p (c i) j -> p c j i", i=4),
+            w3_raw[:].rearrange("p j (c i) -> p c j i", i=4),
+            1.0,
+            0.0,
+            ALU.mult,
+            ALU.add,
+        )
+        early, late = (0, 1), (2, 3)
+        first_round(early)
+        fetch(early, 0, HALF)
+        fetch(early, HALF, S)
+        first_round(late)
+        fetch(late, 0, HALF)
+        fetch(late, HALF, S)
+        second_round(early, 0, S)
+        w3_codes, w3_scales = quantize("q3", g3[:].rearrange("p n j -> p (n j)"))
         for n, (j0, j1) in enumerate(TAIL):
             width = j1 - j0
-            cu4 = keep.tile([P, PACK, width], F32, name=f"cu4_{n}")
-            db = keep.tile([P, PACK, width], F32, name=f"db{n}")
-            via2 = keep.tile([P, PACK, width], F32, name=f"via2_{n}")
-            d2 = keep.tile([P, PACK, width], F32, name=f"d2_{n}")
-            hid = keep.tile([P, PACK, width], BF16, name=f"hid{n}")
             hid_g = keep.tile([P, width, PACK], BF16, name=f"hid_g{n}", align_bytes=64)
             res = keep.tile([P, width], F32, name=f"res{n}")
-            for t in range(PACK):
-                nc.scalar.activation(cu4[:, t, :], wgt[t][:].indirect(entries(u1_sb, j0, j1)), ACT.Copy, scale=0.4)
-            for t in range(PACK):
-                nc.scalar.activation(db[:, t, :], d1[:, t, :].indirect(entries(u2_sb, j0, j1)), ACT.Copy)
-            for a in (0, 2):
-                nc.vector.tensor_tensor(via2[:, a : a + 2], db[:, a : a + 2], cu4[:, a : a + 2], ALU.add)
-            for a in (0, 2):
-                nc.vector.tensor_tensor(d2[:, a : a + 2], via2[:, a : a + 2], d1[:, a : a + 2, j0:j1], ALU.min)
-            for t in range(PACK):
-                nc.vector.scalar_tensor_tensor(
-                    hid[:, t, :], d2[:, t, :], unit15[:, t : t + 1], d0u[:, t, j0:j1], ALU.mult, ALU.subtract
-                )
+            second_round(late, j0, j1)
             nc.scalar.copy(
                 hid_g[:].rearrange("p (c i) t -> p c t i", i=4),
-                hid[:].rearrange("p t (c i) -> p c t i", i=4),
+                hid[:, :, j0:j1].rearrange("p t (c i) -> p c t i", i=4),
             )
             h_codes, h_scales = quantize(f"qh{n}", hid_g[:].rearrange("p c t -> p (c t)"))
             acc = psum.tile([P, width], F32, name=f"acc{n}", tag=f"bank{n}")

@@ -22,6 +22,7 @@ PASSES = K // K_PASS
 LIST = 16
 HALF = S // 2
 SPLIT = 96
+RUN = 4
 LN_FLOOR = 2.0**-62
 TAIL = ((0, 256), (256, 384), (384, 512))
 
@@ -53,7 +54,10 @@ def tile_picked_ybellmf_dist_p_kernel(
         xs_all = keep.tile([P, T], U8, name="xs_all")
         xs_rows = keep.tile([P, T // 4], I32, name="xs_rows")
         nc.vector.memset(xs_all[:].bitcast(I32), 0)
-        unit_sb = keep.tile([P, PACK], F32, name="unit_sb")
+        unit_sb = keep.tile([P, PACK, 8], F32, name="unit_sb")
+        unit_rows = unit.rearrange("(q t b) o -> t q b o", t=PACK, b=RUN)
+        for t in range(PACK):
+            nc.gpsimd.dma_start(unit_sb[:, t, 0:1], unit_rows[t])
 
         for q in range(4):
             rows = slice(32 * q, 32 * q + 4 * PASSES)
@@ -70,15 +74,14 @@ def tile_picked_ybellmf_dist_p_kernel(
         w2_0b = load_weight("w2_0b", w2, 0, H // 2, H)
         w2_1a = load_weight("w2_1a", w2, 1, 0, H // 2)
         w2_1b = load_weight("w2_1b", w2, 1, H // 2, H)
-        nc.sync.dma_start(unit_sb[:], unit.rearrange("(p t) o -> p (t o)", t=PACK))
         u1_sb = load_list("u1_sb", u1)
         u2_sb = load_list("u2_sb", u2)
 
         def deal(copy, grouped, raw, c0):
             m0, m1 = c0 // PACK, (c0 + raw.shape[2]) // PACK
             copy(
-                grouped[:, :, m0:m1, :].rearrange("p t m j -> p m j t"),
-                raw.rearrange("p j (m t) -> p m j t", t=PACK),
+                grouped[:, :, m0:m1, :].rearrange("p t (q b) j -> p t q j b", b=RUN),
+                raw.rearrange("p j (q t b) -> p t q j b", t=PACK, b=RUN),
             )
 
         def grouped_tile(name):
@@ -160,12 +163,15 @@ def tile_picked_ybellmf_dist_p_kernel(
         deal(nc.vector.tensor_copy, g21, w2_1a[:], 0)
         deal(nc.vector.tensor_copy, g21, w2_1b[:], H // 2)
         second_pass("q21", g21, yw)
-        w3_raw = load_weight("w3_raw", w3, 0, 0, N, tag="w2_1b")
+        w3_raw = keep.tile([P, PACK, N], F32, name="w3_raw", tag="w2_1b")
+        w3_rows = w3.rearrange("(q t b) n -> t q b n", t=PACK, b=RUN)
+        for t in range(PACK):
+            nc.sync.dma_start(w3_raw[:, t, :], w3_rows[t])
 
         unit15 = keep.tile([P, PACK], F32, name="unit15")
-        nc.vector.tensor_scalar(unit15[:], unit_sb[:], 1.5, None, ALU.mult)
         unit05 = keep.tile([P, PACK], F32, name="unit05")
-        nc.vector.tensor_scalar(unit05[:], unit_sb[:], 0.5, None, ALU.mult)
+        nc.vector.tensor_scalar(unit15[:], unit_sb[:, :, 0], 1.5, None, ALU.mult)
+        nc.vector.tensor_scalar(unit05[:], unit_sb[:, :, 0], 0.5, None, ALU.mult)
 
         d0 = [keep.tile([P, S], F32, name=f"d0_{t}") for t in range(PACK)]
         da = keep.tile([P, PACK, S], F32, name="da")

@@ -24,7 +24,7 @@ HALF = S // 2
 SPLIT = 96
 RUN = 4
 LN_FLOOR = 2.0**-62
-TAIL = ((0, 256), (256, 384), (384, 512))
+TAIL = ((0, 256, 256), (256, 512, 112))
 
 
 def tile_picked_ybellmf_dist_p_kernel(
@@ -55,9 +55,6 @@ def tile_picked_ybellmf_dist_p_kernel(
         xs_rows = keep.tile([P, T // 4], I32, name="xs_rows")
         nc.vector.memset(xs_all[:].bitcast(I32), 0)
         unit_sb = keep.tile([P, PACK, 8], F32, name="unit_sb")
-        unit_rows = unit.rearrange("(q t b) o -> t q b o", t=PACK, b=RUN)
-        for t in range(PACK):
-            nc.gpsimd.dma_start(unit_sb[:, t, 0:1], unit_rows[t])
 
         for q in range(4):
             rows = slice(32 * q, 32 * q + 4 * PASSES)
@@ -76,12 +73,15 @@ def tile_picked_ybellmf_dist_p_kernel(
         w2_1b = load_weight("w2_1b", w2, 1, H // 2, H)
         u1_sb = load_list("u1_sb", u1)
         u2_sb = load_list("u2_sb", u2)
+        unit_rows = unit.rearrange("(q t b) o -> t q b o", t=PACK, b=RUN)
+        for t in range(PACK):
+            nc.sync.dma_start(unit_sb[:, t, 0:1], unit_rows[t])
 
-        def deal(copy, grouped, raw, c0):
+        def deal(copy, grouped, raw, c0, tiles=slice(0, PACK)):
             m0, m1 = c0 // PACK, (c0 + raw.shape[2]) // PACK
             copy(
-                grouped[:, :, m0:m1, :].rearrange("p t (q b) j -> p t q j b", b=RUN),
-                raw.rearrange("p j (q t b) -> p t q j b", t=PACK, b=RUN),
+                grouped[:, tiles, m0:m1, :].rearrange("p t (q b) j -> p t q j b", b=RUN),
+                raw.rearrange("p j (q t b) -> p t q j b", t=PACK, b=RUN)[:, tiles],
             )
 
         def grouped_tile(name):
@@ -118,8 +118,11 @@ def tile_picked_ybellmf_dist_p_kernel(
             for t in range(PACK):
                 product(banks[t], codes[:, t * P : (t + 1) * P], scales[:, t * P : (t + 1) * P], 0)
 
-        def second_pass(name, grouped, banks):
+        def second_pass(name, grouped, last, banks):
+            deal(nc.vector.tensor_copy, grouped, last[:], H // 2, slice(0, 1))
             for t in range(PACK):
+                if t + 1 < PACK:
+                    deal(nc.vector.tensor_copy, grouped, last[:], H // 2, slice(t + 1, t + 2))
                 codes, scales = quantize(f"{name}_{t}", grouped[:, t].rearrange("p m j -> p (m j)"))
                 product(banks[t], codes[:], scales[:], 1)
 
@@ -149,10 +152,8 @@ def tile_picked_ybellmf_dist_p_kernel(
         first_pass("q10", g10, y)
         gather_words(1, x_all1)
         g11 = grouped_tile("g11")
-        deal(nc.scalar.copy, g11, w1_1a[:, :, :SPLIT], 0)
-        deal(nc.vector.tensor_copy, g11, w1_1a[:, :, SPLIT:], SPLIT)
-        deal(nc.vector.tensor_copy, g11, w1_1b[:], H // 2)
-        second_pass("q11", g11, y)
+        deal(nc.vector.tensor_copy, g11, w1_1a[:], 0)
+        second_pass("q11", g11, w1_1b, y)
         log_y = log_sigmoid("y", y)
 
         g20 = grouped_tile("g20")
@@ -161,8 +162,7 @@ def tile_picked_ybellmf_dist_p_kernel(
         first_pass("q20", g20, yw)
         g21 = grouped_tile("g21")
         deal(nc.vector.tensor_copy, g21, w2_1a[:], 0)
-        deal(nc.vector.tensor_copy, g21, w2_1b[:], H // 2)
-        second_pass("q21", g21, yw)
+        second_pass("q21", g21, w2_1b, yw)
         w3_raw = keep.tile([P, PACK, N], F32, name="w3_raw", tag="w2_1b")
         w3_rows = w3.rearrange("(q t b) n -> t q b n", t=PACK, b=RUN)
         for t in range(PACK):
@@ -170,8 +170,8 @@ def tile_picked_ybellmf_dist_p_kernel(
 
         unit15 = keep.tile([P, PACK], F32, name="unit15")
         unit05 = keep.tile([P, PACK], F32, name="unit05")
-        nc.vector.tensor_scalar(unit15[:], unit_sb[:, :, 0], 1.5, None, ALU.mult)
-        nc.vector.tensor_scalar(unit05[:], unit_sb[:, :, 0], 0.5, None, ALU.mult)
+        nc.gpsimd.tensor_scalar(unit05[:], unit_sb[:, :, 0], 0.5, 0.0, ALU.mult, ALU.add)
+        nc.gpsimd.tensor_scalar(unit15[:], unit_sb[:, :, 0], 1.5, 0.0, ALU.mult, ALU.add)
 
         d0 = [keep.tile([P, S], F32, name=f"d0_{t}") for t in range(PACK)]
         da = keep.tile([P, PACK, S], F32, name="da")
@@ -236,15 +236,17 @@ def tile_picked_ybellmf_dist_p_kernel(
         fetch(late, HALF, S)
         second_round(early, 0, S)
         w3_codes, w3_scales = quantize("q3", g3[:].rearrange("p n j -> p (n j)"))
-        for n, (j0, j1) in enumerate(TAIL):
+        for n, (j0, j1, share) in enumerate(TAIL):
             width = j1 - j0
             hid_g = keep.tile([P, width, PACK], BF16, name=f"hid_g{n}", align_bytes=64)
             res = keep.tile([P, width], F32, name=f"res{n}")
             second_round(late, j0, j1)
-            nc.scalar.copy(
-                hid_g[:].rearrange("p (c i) t -> p c t i", i=4),
-                hid[:, :, j0:j1].rearrange("p t (c i) -> p c t i", i=4),
-            )
+            for copy, c0, c1 in ((nc.scalar.copy, 0, share), (nc.vector.tensor_copy, share, width)):
+                if c0 < c1:
+                    copy(
+                        hid_g[:, c0:c1].rearrange("p (c i) t -> p c t i", i=4),
+                        hid[:, :, j0 + c0 : j0 + c1].rearrange("p t (c i) -> p c t i", i=4),
+                    )
             h_codes, h_scales = quantize(f"qh{n}", hid_g[:].rearrange("p c t -> p (c t)"))
             acc = psum.tile([P, width], F32, name=f"acc{n}", tag=f"bank{n}")
             nc.tensor.matmul_mx(

@@ -19,12 +19,14 @@ P = 128
 PACK = 4
 K_PASS = P * PACK
 PASSES = K // K_PASS
+RUN = 4
+QUADRANT = 32
+SCALE_ROWS = 4
 LIST = 16
 HALF = S // 2
-SPLIT = 96
-RUN = 4
+QUARTER = S // 4
+DMA_BLOCK = 8
 LN_FLOOR = 2.0**-62
-TAIL = ((0, 256, 256), (256, 512, 112))
 
 
 def tile_picked_ybellmf_dist_p_kernel(
@@ -41,51 +43,38 @@ def tile_picked_ybellmf_dist_p_kernel(
             return tile
 
         def load_words(g):
-            tile = keep.tile([P, T], I32, name=f"x_all{g}")
+            tile = keep.tile([P, T], I32, name=f"x_table{g}")
             nc.sync.dma_start(tile[:], x_words[g].rearrange("p n r -> p (n r)").bitcast(I32))
             return tile
 
-        def load_weight(name, w, g, c0, c1, tag=None):
-            tile = keep.tile([P, PACK, c1 - c0], F32, name=name, tag=tag or name)
-            rows = w[g * K_PASS : (g + 1) * K_PASS, c0:c1]
-            nc.sync.dma_start(tile[:], rows.rearrange("(p j) c -> p j c", j=PACK))
+        def load_weight(name, w, g):
+            tile = keep.tile([P, PACK, H], F32, name=name)
+            rows = w[g * K_PASS : (g + 1) * K_PASS, :].rearrange("(p j) c -> p j c", j=PACK)
+            for j in range(0, PACK, 2):
+                nc.sync.dma_start(tile[:, j : j + 2, :], rows[:, j : j + 2, :])
             return tile
 
-        xs_all = keep.tile([P, T], U8, name="xs_all")
-        xs_rows = keep.tile([P, T // 4], I32, name="xs_rows")
-        nc.vector.memset(xs_all[:].bitcast(I32), 0)
-        unit_sb = keep.tile([P, PACK, 8], F32, name="unit_sb")
-
-        for q in range(4):
-            rows = slice(32 * q, 32 * q + 4 * PASSES)
-            nc.sync.dma_start(xs_rows[rows, :], x_scales[:, 4 * q : 4 * q + 4, :].bitcast(I32))
-            nc.vector.tensor_copy(xs_all[rows, :].bitcast(I32), xs_rows[rows, :])
+        scale_table = keep.tile([P, T], U8, name="scale_table")
+        scale_rows = keep.tile([P, T // 4], I32, name="scale_rows")
+        nc.vector.memset(scale_table[:].bitcast(I32), 0)
+        for quad in range(P // QUADRANT):
+            live = slice(QUADRANT * quad, QUADRANT * quad + SCALE_ROWS * PASSES)
+            rows = x_scales[:, SCALE_ROWS * quad : SCALE_ROWS * (quad + 1), :]
+            nc.sync.dma_start(scale_rows[live, :], rows.bitcast(I32))
+            nc.vector.tensor_copy(scale_table[live, :].bitcast(I32), scale_rows[live, :])
         offs_sb = load_list("offs_sb", offs)
-        w1_0a = load_weight("w1_0a", w1, 0, 0, H // 2)
-        x_all0 = load_words(0)
-        w1_0b = load_weight("w1_0b", w1, 0, H // 2, H)
-        x_all1 = load_words(1)
-        w1_1a = load_weight("w1_1a", w1, 1, 0, H // 2)
-        w1_1b = load_weight("w1_1b", w1, 1, H // 2, H)
-        w2_0a = load_weight("w2_0a", w2, 0, 0, H // 2)
-        w2_0b = load_weight("w2_0b", w2, 0, H // 2, H)
-        w2_1a = load_weight("w2_1a", w2, 1, 0, H // 2)
-        w2_1b = load_weight("w2_1b", w2, 1, H // 2, H)
+        x_table0 = load_words(0)
+        w1_raw0 = load_weight("w1_raw0", w1, 0)
+        x_table1 = load_words(1)
+        w1_raw1 = load_weight("w1_raw1", w1, 1)
+        w2_raw0 = load_weight("w2_raw0", w2, 0)
+        w2_raw1 = load_weight("w2_raw1", w2, 1)
         u1_sb = load_list("u1_sb", u1)
         u2_sb = load_list("u2_sb", u2)
+        unit_sb = keep.tile([P, PACK, DMA_BLOCK], F32, name="unit_sb")
         unit_rows = unit.rearrange("(q t b) o -> t q b o", t=PACK, b=RUN)
         for t in range(PACK):
             nc.sync.dma_start(unit_sb[:, t, 0:1], unit_rows[t])
-
-        def deal(copy, grouped, raw, c0, tiles=slice(0, PACK)):
-            m0, m1 = c0 // PACK, (c0 + raw.shape[2]) // PACK
-            copy(
-                grouped[:, tiles, m0:m1, :].rearrange("p t (q b) j -> p t q j b", b=RUN),
-                raw.rearrange("p j (q t b) -> p t q j b", t=PACK, b=RUN)[:, tiles],
-            )
-
-        def grouped_tile(name):
-            return keep.tile([P, PACK, P, PACK], BF16, name=name, align_bytes=64)
 
         def quantize(name, src):
             width = src.shape[1] // PACK
@@ -94,37 +83,34 @@ def tile_picked_ybellmf_dist_p_kernel(
             nc.vector.quantize_mx(out=codes[:].bitcast(FP8X4), scales=scales[:], in_=src)
             return codes, scales
 
-        x_codes = []
-        x_sc = keep.tile([P, S], U8, name="x_sc", align_bytes=64)
+        def gather_words(name, table):
+            codes = keep.tile([P, S], U32, name=name, align_bytes=64)
+            nc.vector.tensor_copy(codes[:], table[:].bitcast(U32).indirect(offs_sb[:]))
+            return codes
 
-        def gather_words(g, x_all):
-            tile = keep.tile([P, S], U32, name=f"x_codes{g}", align_bytes=64)
-            nc.vector.tensor_copy(tile[:], x_all[:].bitcast(U32).indirect(offs_sb[:]))
-            x_codes.append(tile)
+        def weight_pass(name, raw, g, x_codes, banks):
+            dealt = keep.tile([P, PACK, P, PACK], BF16, name=name + "_dealt", align_bytes=64)
 
-        def product(bank, codes, scales, g):
-            nc.tensor.matmul_mx(
-                out=bank[:],
-                lhsT=codes.bitcast(FP8X4),
-                lhsT_scale=scales,
-                rhs=x_codes[g][:].bitcast(FP8X4),
-                rhs_scale=x_sc[4 * g : P, :],
-                start=(g == 0),
-                stop=(g == PASSES - 1),
-            )
+            def deal(t):
+                nc.vector.tensor_copy(
+                    dealt[:, t].rearrange("p (q b) j -> p q j b", b=RUN),
+                    raw[:].rearrange("p j (q t b) -> p t q j b", t=PACK, b=RUN)[:, t],
+                )
 
-        def first_pass(name, grouped, banks):
-            codes, scales = quantize(name, grouped[:].rearrange("p t m j -> p (t m j)"))
-            for t in range(PACK):
-                product(banks[t], codes[:, t * P : (t + 1) * P], scales[:, t * P : (t + 1) * P], 0)
-
-        def second_pass(name, grouped, last, banks):
-            deal(nc.vector.tensor_copy, grouped, last[:], H // 2, slice(0, 1))
+            deal(0)
             for t in range(PACK):
                 if t + 1 < PACK:
-                    deal(nc.vector.tensor_copy, grouped, last[:], H // 2, slice(t + 1, t + 2))
-                codes, scales = quantize(f"{name}_{t}", grouped[:, t].rearrange("p m j -> p (m j)"))
-                product(banks[t], codes[:], scales[:], 1)
+                    deal(t + 1)
+                codes, scales = quantize(f"{name}_{t}", dealt[:, t].rearrange("p m j -> p (m j)"))
+                nc.tensor.matmul_mx(
+                    out=banks[t][:],
+                    lhsT=codes[:].bitcast(FP8X4),
+                    lhsT_scale=scales[:],
+                    rhs=x_codes[:].bitcast(FP8X4),
+                    rhs_scale=x_sc[SCALE_ROWS * g : P, :],
+                    start=(g == 0),
+                    stop=(g == PASSES - 1),
+                )
 
         def log_sigmoid(name, banks):
             sig = keep.tile([P, PACK, S], F32, name=name + "_sig")
@@ -136,48 +122,37 @@ def tile_picked_ybellmf_dist_p_kernel(
             return log
 
         def softplus(dst, log, bank):
-            nc.vector.scalar_tensor_tensor(dst, log, -1.0, bank[:], ALU.mult, ALU.max)
+            nc.vector.scalar_tensor_tensor(dst[:], log, -1.0, bank[:], ALU.mult, ALU.max)
 
         def entries(lst, j0, j1):
             return lst[:, j0 // LIST : j1 // LIST]
 
         y = [psum.tile([P, S], F32, name=f"y{t}", tag=f"bank{t}") for t in range(PACK)]
         yw = [psum.tile([P, S], F32, name=f"yw{t}", tag=f"bank{PACK + t}") for t in range(PACK)]
-        nc.vector.tensor_copy(x_sc[:], xs_all[:].indirect(offs_sb[:]))
-        g10 = grouped_tile("g10")
-        deal(nc.scalar.copy, g10, w1_0a[:], 0)
-        gather_words(0, x_all0)
-        deal(nc.scalar.copy, g10, w1_0b[:, :, :SPLIT], H // 2)
-        deal(nc.vector.tensor_copy, g10, w1_0b[:, :, SPLIT:], H // 2 + SPLIT)
-        first_pass("q10", g10, y)
-        gather_words(1, x_all1)
-        g11 = grouped_tile("g11")
-        deal(nc.vector.tensor_copy, g11, w1_1a[:], 0)
-        second_pass("q11", g11, w1_1b, y)
+        x_sc = keep.tile([P, S], U8, name="x_sc", align_bytes=64)
+        nc.vector.tensor_copy(x_sc[:], scale_table[:].indirect(offs_sb[:]))
+        x_codes0 = gather_words("x_codes0", x_table0)
+        weight_pass("w1_0", w1_raw0, 0, x_codes0, y)
+        x_codes1 = gather_words("x_codes1", x_table1)
+        weight_pass("w1_1", w1_raw1, 1, x_codes1, y)
         log_y = log_sigmoid("y", y)
+        weight_pass("w2_0", w2_raw0, 0, x_codes0, yw)
+        weight_pass("w2_1", w2_raw1, 1, x_codes1, yw)
 
-        g20 = grouped_tile("g20")
-        deal(nc.vector.tensor_copy, g20, w2_0a[:], 0)
-        deal(nc.vector.tensor_copy, g20, w2_0b[:], H // 2)
-        first_pass("q20", g20, yw)
-        g21 = grouped_tile("g21")
-        deal(nc.vector.tensor_copy, g21, w2_1a[:], 0)
-        second_pass("q21", g21, w2_1b, yw)
-        w3_raw = keep.tile([P, PACK, N], F32, name="w3_raw", tag="w2_1b")
+        w3_raw = keep.tile([P, PACK, N], F32, name="w3_raw", tag="w2_raw1")
         w3_rows = w3.rearrange("(q t b) n -> t q b n", t=PACK, b=RUN)
         for t in range(PACK):
             nc.sync.dma_start(w3_raw[:, t, :], w3_rows[t])
 
-        unit15 = keep.tile([P, PACK], F32, name="unit15")
         unit05 = keep.tile([P, PACK], F32, name="unit05")
+        unit15 = keep.tile([P, PACK], F32, name="unit15")
         nc.gpsimd.tensor_scalar(unit05[:], unit_sb[:, :, 0], 0.5, 0.0, ALU.mult, ALU.add)
         nc.gpsimd.tensor_scalar(unit15[:], unit_sb[:, :, 0], 1.5, 0.0, ALU.mult, ALU.add)
-
         d0 = [keep.tile([P, S], F32, name=f"d0_{t}") for t in range(PACK)]
         da = keep.tile([P, PACK, S], F32, name="da")
         d0u = keep.tile([P, PACK, S], F32, name="d0u")
         for t in range(PACK):
-            softplus(d0[t][:], log_y[:, t, :], y[t])
+            softplus(d0[t], log_y[:, t, :], y[t])
         for t in range(PACK):
             for j0 in (0, HALF):
                 nc.vector.tensor_copy(da[:, t, j0 : j0 + HALF], d0[t][:].indirect(entries(u1_sb, j0, j0 + HALF)))
@@ -196,7 +171,7 @@ def tile_picked_ybellmf_dist_p_kernel(
 
         def first_round(pair):
             for t in pair:
-                softplus(wgt[t][:], log_w[:, t, :], yw[t])
+                softplus(wgt[t], log_w[:, t, :], yw[t])
             for t in pair:
                 nc.vector.scalar_tensor_tensor(via1[:, t, :], wgt[t][:], 0.4, da[:, t, :], ALU.mult, ALU.add)
             for t in pair:
@@ -218,45 +193,48 @@ def tile_picked_ybellmf_dist_p_kernel(
                     hid[:, t, j0:j1], d2[:, t, j0:j1], unit15[:, t : t + 1], d0u[:, t, j0:j1], ALU.mult, ALU.subtract
                 )
 
-        g3 = keep.tile([P, N, PACK], BF16, name="g3", align_bytes=64)
+        w3_woven = keep.tile([P, N, PACK], BF16, name="w3_woven", align_bytes=64)
         nc.gpsimd.tensor_scalar(
-            g3[:].rearrange("p (c i) j -> p c j i", i=4),
-            w3_raw[:].rearrange("p j (c i) -> p c j i", i=4),
+            w3_woven[:].rearrange("p (c i) t -> p c t i", i=RUN),
+            w3_raw[:].rearrange("p t (c i) -> p c t i", i=RUN),
             1.0,
             0.0,
             ALU.mult,
             ALU.add,
         )
+
         early, late = (0, 1), (2, 3)
-        first_round(early)
-        fetch(early, 0, HALF)
-        fetch(early, HALF, S)
-        first_round(late)
-        fetch(late, 0, HALF)
-        fetch(late, HALF, S)
+        for pair in (early, late):
+            first_round(pair)
+            fetch(pair, 0, HALF)
+            fetch(pair, HALF, S)
         second_round(early, 0, S)
-        w3_codes, w3_scales = quantize("q3", g3[:].rearrange("p n j -> p (n j)"))
-        for n, (j0, j1, share) in enumerate(TAIL):
+        w3_codes, w3_scales = quantize("w3", w3_woven[:].rearrange("p n t -> p (n t)"))
+
+        def finish(j0, j1, copy, bank):
             width = j1 - j0
-            hid_g = keep.tile([P, width, PACK], BF16, name=f"hid_g{n}", align_bytes=64)
-            res = keep.tile([P, width], F32, name=f"res{n}")
-            second_round(late, j0, j1)
-            for copy, c0, c1 in ((nc.scalar.copy, 0, share), (nc.vector.tensor_copy, share, width)):
-                if c0 < c1:
-                    copy(
-                        hid_g[:, c0:c1].rearrange("p (c i) t -> p c t i", i=4),
-                        hid[:, :, j0 + c0 : j0 + c1].rearrange("p t (c i) -> p c t i", i=4),
-                    )
-            h_codes, h_scales = quantize(f"qh{n}", hid_g[:].rearrange("p c t -> p (c t)"))
-            acc = psum.tile([P, width], F32, name=f"acc{n}", tag=f"bank{n}")
+            woven = keep.tile([P, width, PACK], BF16, name=f"woven{j0}", align_bytes=64)
+            copy(
+                woven[:].rearrange("p (c i) t -> p c t i", i=RUN),
+                hid[:, :, j0:j1].rearrange("p t (c i) -> p c t i", i=RUN),
+            )
+            codes, scales = quantize(f"hid{j0}", woven[:].rearrange("p c t -> p (c t)"))
+            acc = psum.tile([P, width], F32, name=f"acc{j0}", tag=f"bank{bank}")
             nc.tensor.matmul_mx(
                 out=acc[:],
                 lhsT=w3_codes[:].bitcast(FP8X4),
                 lhsT_scale=w3_scales[:],
-                rhs=h_codes[:].bitcast(FP8X4),
-                rhs_scale=h_scales[:],
+                rhs=codes[:].bitcast(FP8X4),
+                rhs_scale=scales[:],
                 start=True,
                 stop=True,
             )
-            nc.scalar.copy(res[:], acc[:])
+            res = keep.tile([P, width], F32, name=f"res{j0}")
+            copy(res[:], acc[:])
             nc.sync.dma_start(out[:, j0:j1], res[:])
+
+        second_round(late, 0, HALF)
+        finish(0, HALF, nc.scalar.copy, 0)
+        second_round(late, HALF, S)
+        finish(HALF, HALF + QUARTER, nc.scalar.copy, 1)
+        finish(HALF + QUARTER, S, nc.vector.tensor_copy, 2)

from contextlib import ExitStack

import concourse.mybir as mybir

K, T, S, N, H = 1024, 1024, 512, 128, 512
FLOPS = 2 * (2 * K * H * S + H * N * S)

F32 = mybir.dt.float32
BF16 = mybir.dt.bfloat16
I32 = mybir.dt.int32
U32 = mybir.dt.uint32
U16 = mybir.dt.uint16
U8 = mybir.dt.uint8
FP8X4 = mybir.dt.float8_e4m3fn_x4
ALU = mybir.AluOpType
ACT = mybir.ActivationFunctionType

P = 128
PACK = 4
K_PASS = P * PACK
PASSES = K // K_PASS
RUN = 4
QUADRANT = 32
SCALE_ROWS = 4
LIST = 16
HALF = S // 2
QUARTER = S // 4
DMA_BLOCK = 8
LN_FLOOR = 2.0**-62


def tile_picked_ybellmf_dist_p_kernel(
    tc, x_words, x_scales, w1, w2, unit, w3, offs, u1, u2, out
):
    nc = tc.nc
    with ExitStack() as ctx:
        keep = ctx.enter_context(tc.tile_pool(name="keep", bufs=1))
        psum = ctx.enter_context(tc.psum_pool(name="psum", bufs=1))

        def load_list(name, src):
            tile = keep.tile([P, S // LIST], U16, name=name)
            nc.sync.dma_start(tile[:], src)
            return tile

        def load_words(g):
            tile = keep.tile([P, T], I32, name=f"x_table{g}")
            nc.sync.dma_start(tile[:], x_words[g].rearrange("p n r -> p (n r)").bitcast(I32))
            return tile

        def load_weight(name, w, g):
            tile = keep.tile([P, PACK, H], F32, name=name)
            rows = w[g * K_PASS : (g + 1) * K_PASS, :].rearrange("(p j) c -> p j c", j=PACK)
            for j in range(0, PACK, 2):
                nc.sync.dma_start(tile[:, j : j + 2, :], rows[:, j : j + 2, :])
            return tile

        scale_table = keep.tile([P, T], U8, name="scale_table")
        scale_rows = keep.tile([P, T // 4], I32, name="scale_rows")
        nc.vector.memset(scale_table[:].bitcast(I32), 0)
        for quad in range(P // QUADRANT):
            live = slice(QUADRANT * quad, QUADRANT * quad + SCALE_ROWS * PASSES)
            rows = x_scales[:, SCALE_ROWS * quad : SCALE_ROWS * (quad + 1), :]
            nc.sync.dma_start(scale_rows[live, :], rows.bitcast(I32))
            nc.vector.tensor_copy(scale_table[live, :].bitcast(I32), scale_rows[live, :])
        offs_sb = load_list("offs_sb", offs)
        x_table0 = load_words(0)
        w1_raw0 = load_weight("w1_raw0", w1, 0)
        x_table1 = load_words(1)
        w1_raw1 = load_weight("w1_raw1", w1, 1)
        w2_raw0 = load_weight("w2_raw0", w2, 0)
        w2_raw1 = load_weight("w2_raw1", w2, 1)
        u1_sb = load_list("u1_sb", u1)
        u2_sb = load_list("u2_sb", u2)
        unit_sb = keep.tile([P, PACK, DMA_BLOCK], F32, name="unit_sb")
        unit_rows = unit.rearrange("(q t b) o -> t q b o", t=PACK, b=RUN)
        for t in range(PACK):
            nc.sync.dma_start(unit_sb[:, t, 0:1], unit_rows[t])

        def quantize(name, src):
            width = src.shape[1] // PACK
            codes = keep.tile([P, width], U32, name=name + "_codes", align_bytes=64)
            scales = keep.tile([P, width], U8, name=name + "_scales", align_bytes=64)
            nc.vector.quantize_mx(out=codes[:].bitcast(FP8X4), scales=scales[:], in_=src)
            return codes, scales

        def gather_words(name, table):
            codes = keep.tile([P, S], U32, name=name, align_bytes=64)
            nc.vector.tensor_copy(codes[:], table[:].bitcast(U32).indirect(offs_sb[:]))
            return codes

        def weight_pass(name, raw, g, x_codes, banks):
            dealt = keep.tile([P, PACK, P, PACK], BF16, name=name + "_dealt", align_bytes=64)

            def deal(t):
                nc.vector.tensor_copy(
                    dealt[:, t].rearrange("p (q b) j -> p q j b", b=RUN),
                    raw[:].rearrange("p j (q t b) -> p t q j b", t=PACK, b=RUN)[:, t],
                )

            deal(0)
            for t in range(PACK):
                if t + 1 < PACK:
                    deal(t + 1)
                codes, scales = quantize(f"{name}_{t}", dealt[:, t].rearrange("p m j -> p (m j)"))
                nc.tensor.matmul_mx(
                    out=banks[t][:],
                    lhsT=codes[:].bitcast(FP8X4),
                    lhsT_scale=scales[:],
                    rhs=x_codes[:].bitcast(FP8X4),
                    rhs_scale=x_sc[SCALE_ROWS * g : P, :],
                    start=(g == 0),
                    stop=(g == PASSES - 1),
                )

        def log_sigmoid(name, banks):
            sig = keep.tile([P, PACK, S], F32, name=name + "_sig")
            log = keep.tile([P, PACK, S], F32, name=name + "_log")
            for t in range(PACK):
                nc.scalar.activation(sig[:, t, :], banks[t][:], ACT.Sigmoid, scale=-1.0)
            for t in range(PACK):
                nc.scalar.activation(log[:, t, :], sig[:, t, :], ACT.Ln, bias=LN_FLOOR)
            return log

        def softplus(dst, log, bank):
            nc.vector.scalar_tensor_tensor(dst[:], log, -1.0, bank[:], ALU.mult, ALU.max)

        def entries(lst, j0, j1):
            return lst[:, j0 // LIST : j1 // LIST]

        y = [psum.tile([P, S], F32, name=f"y{t}", tag=f"bank{t}") for t in range(PACK)]
        yw = [psum.tile([P, S], F32, name=f"yw{t}", tag=f"bank{PACK + t}") for t in range(PACK)]
        x_sc = keep.tile([P, S], U8, name="x_sc", align_bytes=64)
        nc.vector.tensor_copy(x_sc[:], scale_table[:].indirect(offs_sb[:]))
        x_codes0 = gather_words("x_codes0", x_table0)
        weight_pass("w1_0", w1_raw0, 0, x_codes0, y)
        x_codes1 = gather_words("x_codes1", x_table1)
        weight_pass("w1_1", w1_raw1, 1, x_codes1, y)
        log_y = log_sigmoid("y", y)
        weight_pass("w2_0", w2_raw0, 0, x_codes0, yw)
        weight_pass("w2_1", w2_raw1, 1, x_codes1, yw)

        w3_raw = keep.tile([P, PACK, N], F32, name="w3_raw", tag="w2_raw1")
        w3_rows = w3.rearrange("(q t b) n -> t q b n", t=PACK, b=RUN)
        for t in range(PACK):
            nc.sync.dma_start(w3_raw[:, t, :], w3_rows[t])

        unit05 = keep.tile([P, PACK], F32, name="unit05")
        unit15 = keep.tile([P, PACK], F32, name="unit15")
        nc.gpsimd.tensor_scalar(unit05[:], unit_sb[:, :, 0], 0.5, 0.0, ALU.mult, ALU.add)
        nc.gpsimd.tensor_scalar(unit15[:], unit_sb[:, :, 0], 1.5, 0.0, ALU.mult, ALU.add)
        d0 = [keep.tile([P, S], F32, name=f"d0_{t}") for t in range(PACK)]
        da = keep.tile([P, PACK, S], F32, name="da")
        d0u = keep.tile([P, PACK, S], F32, name="d0u")
        for t in range(PACK):
            softplus(d0[t], log_y[:, t, :], y[t])
        for t in range(PACK):
            for j0 in (0, HALF):
                nc.vector.tensor_copy(da[:, t, j0 : j0 + HALF], d0[t][:].indirect(entries(u1_sb, j0, j0 + HALF)))
        for t in range(PACK):
            nc.gpsimd.tensor_scalar(d0u[:, t, :], d0[t][:], unit05[:, t : t + 1], 0.0, ALU.mult, ALU.add)

        log_w = log_sigmoid("yw", yw)
        wgt = [keep.tile([P, S], F32, name=f"wgt_{t}") for t in range(PACK)]
        via1 = keep.tile([P, PACK, S], F32, name="via1")
        d1 = keep.tile([P, PACK, S], F32, name="d1")
        cu4 = keep.tile([P, PACK, S], F32, name="cu4")
        db = keep.tile([P, PACK, S], F32, name="db")
        via2 = keep.tile([P, PACK, S], F32, name="via2")
        d2 = keep.tile([P, PACK, S], F32, name="d2")
        hid = keep.tile([P, PACK, S], BF16, name="hid")

        def first_round(pair):
            for t in pair:
                softplus(wgt[t], log_w[:, t, :], yw[t])
            for t in pair:
                nc.vector.scalar_tensor_tensor(via1[:, t, :], wgt[t][:], 0.4, da[:, t, :], ALU.mult, ALU.add)
            for t in pair:
                nc.vector.tensor_tensor(d1[:, t, :], via1[:, t, :], d0[t][:], ALU.min)

        def fetch(pair, j0, j1):
            for t in pair:
                nc.scalar.activation(cu4[:, t, j0:j1], wgt[t][:].indirect(entries(u1_sb, j0, j1)), ACT.Copy, scale=0.4)
            for t in pair:
                nc.scalar.activation(db[:, t, j0:j1], d1[:, t, :].indirect(entries(u2_sb, j0, j1)), ACT.Copy)

        def second_round(pair, j0, j1):
            for t in pair:
                nc.vector.tensor_tensor(via2[:, t, j0:j1], db[:, t, j0:j1], cu4[:, t, j0:j1], ALU.add)
            for t in pair:
                nc.vector.tensor_tensor(d2[:, t, j0:j1], via2[:, t, j0:j1], d1[:, t, j0:j1], ALU.min)
            for t in pair:
                nc.vector.scalar_tensor_tensor(
                    hid[:, t, j0:j1], d2[:, t, j0:j1], unit15[:, t : t + 1], d0u[:, t, j0:j1], ALU.mult, ALU.subtract
                )

        w3_woven = keep.tile([P, N, PACK], BF16, name="w3_woven", align_bytes=64)
        nc.gpsimd.tensor_scalar(
            w3_woven[:].rearrange("p (c i) t -> p c t i", i=RUN),
            w3_raw[:].rearrange("p t (c i) -> p c t i", i=RUN),
            1.0,
            0.0,
            ALU.mult,
            ALU.add,
        )

        early, late = (0, 1), (2, 3)
        for pair in (early, late):
            first_round(pair)
            fetch(pair, 0, HALF)
            fetch(pair, HALF, S)
        second_round(early, 0, S)
        w3_codes, w3_scales = quantize("w3", w3_woven[:].rearrange("p n t -> p (n t)"))

        def finish(j0, j1, copy, bank):
            width = j1 - j0
            woven = keep.tile([P, width, PACK], BF16, name=f"woven{j0}", align_bytes=64)
            copy(
                woven[:].rearrange("p (c i) t -> p c t i", i=RUN),
                hid[:, :, j0:j1].rearrange("p t (c i) -> p c t i", i=RUN),
            )
            codes, scales = quantize(f"hid{j0}", woven[:].rearrange("p c t -> p (c t)"))
            acc = psum.tile([P, width], F32, name=f"acc{j0}", tag=f"bank{bank}")
            nc.tensor.matmul_mx(
                out=acc[:],
                lhsT=w3_codes[:].bitcast(FP8X4),
                lhsT_scale=w3_scales[:],
                rhs=codes[:].bitcast(FP8X4),
                rhs_scale=scales[:],
                start=True,
                stop=True,
            )
            res = keep.tile([P, width], F32, name=f"res{j0}")
            copy(res[:], acc[:])
            nc.sync.dma_start(out[:, j0:j1], res[:])

        second_round(late, 0, HALF)
        finish(0, HALF, nc.scalar.copy, 0)
        second_round(late, HALF, S)
        finish(HALF, HALF + QUARTER, nc.scalar.copy, 1)
        finish(HALF + QUARTER, S, nc.vector.tensor_copy, 2)
